import numpy as np
import ml_dtypes


def mxq(x, axis, fmt="e4m3"):
    dtype, down = {"e4m3": (ml_dtypes.float8_e4m3fn, 7), "e5m2": (ml_dtypes.float8_e5m2, 14)}[fmt]
    v = np.moveaxis(np.asarray(x, np.float32).astype(ml_dtypes.bfloat16).astype(np.float64), axis, -1)
    blocks = v.reshape(v.shape[:-1] + (-1, 32))
    amax = np.abs(blocks).max(-1, keepdims=True)
    byte = np.maximum(np.where(amax > 0, np.frexp(amax)[1] - 1 + 127, 0) - down, 1)
    scale = np.exp2(byte - 127.0)
    codes = (blocks / scale).astype(np.float32).astype(dtype).astype(np.float64)
    return np.moveaxis((codes * scale).reshape(v.shape), -1, axis)


WIDE = False


def mx_kscale(k):
    if not WIDE:
        return np.ones(k)
    levels = np.array([10, -10, 5, -5, 0])
    if k % 512:
        return np.exp2(np.random.permutation(np.resize(levels, k // 32))).repeat(32)
    a = np.empty((k // 512, 16))
    for p in range(k // 512):
        a[p, :8] = np.random.permutation(np.resize(levels, 8))
        for g in range(8):
            far = levels[np.abs(levels - a[p, g]) >= 10]
            a[p, g + 8] = far[np.random.randint(len(far))]
    return np.exp2(a.ravel()).repeat(32)


def f64(x):
    return np.asarray(x).astype(np.float64)


def striped(idx):
    return np.tile(idx.reshape(-1, 16).T, (8, 1)).astype(np.uint16)


def unstriped(offs):
    return offs[:16].T.reshape(-1).astype(np.int64)


def pack_weight(w):
    k, n = w.shape
    w = f64(np.asarray(w, np.float32).astype(ml_dtypes.bfloat16)).reshape(k // 32, 32, n)
    amax = np.abs(w).max(1)
    byte = np.clip(np.where(amax > 0, np.frexp(amax)[1] - 1 + 127 - 7, 1), 1, 254)
    scaled = (w * np.exp2(127.0 - byte)[:, None, :]).reshape(k, n).astype(np.float32)
    words = np.ascontiguousarray(scaled.reshape(k // 512, 128, 4, n).transpose(0, 1, 3, 2)).astype(ml_dtypes.float8_e4m3fn).view(np.uint8)
    return words, np.ascontiguousarray(byte.astype(np.uint8).reshape(k // 512, 16, n))


def unpack_weight(words, scales):
    g, p, n, _ = words.shape
    vals = np.ascontiguousarray(words).view(ml_dtypes.float8_e4m3fn).astype(np.float64) * np.repeat(np.exp2(scales.astype(np.float64) - 127.0), 8, axis=1)[..., None]
    return vals.transpose(0, 1, 3, 2).reshape(g * 512, n)


def relu(v):
    return np.maximum(v, 0.0)


K, T, S, H, N = 1024, 2048, 512, 1024, 128


def setup_inputs():
    n = np.random.standard_normal
    s = mx_kscale(K)[:, None]
    u = mx_kscale(H)
    packed = pack_weight(n((K, T)) * s)
    return {
        "x_words": packed[0],
        "x_scales": packed[1],
        "w1": (n((K, H)) / np.sqrt(K) / s * u).astype(np.float32),
        "w2": (n((H, N)) / np.sqrt(H) / u[:, None]).astype(np.float32),
        "offs": striped(np.random.permutation(T)[:S]),
    }


def reference(x_words, x_scales, w1, w2, offs):
    idx = unstriped(offs)
    xq = unpack_weight(x_words, x_scales)[:, idx]
    h = relu(mxq(f64(w1), 0, "e4m3").T @ xq)
    y = mxq(f64(w2), 0, "e4m3").T @ mxq(h, 0, "e4m3")
    return y

@@ -1,0 +1,211 @@
+from contextlib import ExitStack
+
+import concourse.mybir as mybir
+
+K, T, S, H, N = 1024, 2048, 512, 1024, 128
+FLOPS = 2 * K * H * S + 2 * H * N * S
+
+F32 = mybir.dt.float32
+BF16 = mybir.dt.bfloat16
+I32 = mybir.dt.int32
+U32 = mybir.dt.uint32
+U16 = mybir.dt.uint16
+U8 = mybir.dt.uint8
+FP8X4 = mybir.dt.float8_e4m3fn_x4
+RELU = mybir.ActivationFunctionType.Relu
+
+P = 128
+PACK = 4
+PASS = P * PACK
+BLOCK = 32
+SUB = BLOCK // PACK
+CHUNK = 128
+HALF = PASS // 2
+
+
+def tile_picked_pick_mlp_relu_sub_p_kernel(tc, x_words, x_scales, w1, w2, offs, out):
+    nc = tc.nc
+    k_passes = K // PASS
+    h_passes = H // PASS
+    chunks = S // CHUNK
+
+    with ExitStack() as ctx:
+        keep = ctx.enter_context(tc.tile_pool(name="keep", bufs=1))
+        psum = ctx.enter_context(tc.psum_pool(name="psum", bufs=1))
+
+        def sbuf(name, shape, dtype, reuse=None):
+            return keep.tile(shape, dtype, name=name, tag=reuse or name, align_bytes=64)
+
+        def copy_on(engine, dst, src):
+            if engine == "vector":
+                nc.vector.tensor_copy(out=dst, in_=src)
+            else:
+                nc.scalar.copy(out=dst, in_=src)
+
+        def quantize(name, values, reuse=None):
+            codes = sbuf(name + "_codes", [P, P], U32, reuse)
+            scales = sbuf(name + "_scales", [P, P], U8)
+            nc.vector.quantize_mx(out=codes[:].bitcast(FP8X4), scales=scales[:], in_=values[:])
+            return codes, scales
+
+        offsets = keep.tile([P, S // 16], U16, name="offsets")
+
+        scale_table = sbuf("scale_table", [P, T], U8)
+        nc.vector.memset(scale_table[:].bitcast(I32), 0)
+
+        word_tables = [sbuf("word_table%d" % o, [P, T], I32) for o in range(k_passes)]
+
+        def load_words(o):
+            nc.sync.dma_start(word_tables[o][:], x_words[o].rearrange("p c r -> p (c r)").bitcast(I32))
+
+        nc.sync.dma_start(offsets[:], offs)
+        load_words(0)
+        for quad in range(4):
+            nc.sync.dma_start(
+                scale_table[32 * quad : 32 * quad + 4 * k_passes, :].bitcast(I32),
+                x_scales[:, 4 * quad : 4 * quad + 4, :].bitcast(I32),
+            )
+        load_words(1)
+
+        pieces = [(0, 0, 0, PASS), (0, 1, 0, PASS), (1, 0, 0, HALF), (1, 0, HALF, HALF), (1, 1, 0, HALF), (1, 1, HALF, HALF)]
+        w1_raw = []
+        w2_raw = []
+
+        def load_w1(g, o, first, width):
+            raw = sbuf("w1_raw_%d" % len(w1_raw), [P, PACK, width], F32)
+            cols = slice(g * PASS + first, g * PASS + first + width)
+            nc.sync.dma_start(raw[:], w1[o * PASS : (o + 1) * PASS, cols].rearrange("(p j) c -> p j c", j=PACK))
+            w1_raw.append(raw)
+
+        def load_w2(g, queue):
+            raw = sbuf("w2_raw%d" % g, [P, PACK, N], F32)
+            rows = w2[g * PASS : (g + 1) * PASS, :].rearrange("(b t i) n -> t b i n", t=PACK, i=SUB)
+            for t in range(PACK):
+                queue.dma_start(raw[:, t, :], rows[t])
+            w2_raw.append(raw)
+
+        load_w2(0, nc.sync)
+        for piece in pieces:
+            load_w1(*piece)
+        load_w2(1, nc.sync)
+
+        x_codes = [sbuf("x_codes%d" % o, [P, S], U32) for o in range(k_passes)]
+        x_bytes = sbuf("x_bytes", [P, S], U8)
+        nc.vector.tensor_copy(out=x_codes[0][:], in_=word_tables[0][:].bitcast(U32).indirect(offsets[:]))
+        nc.vector.tensor_copy(out=x_bytes[:], in_=scale_table[:].indirect(offsets[:]))
+        nc.vector.tensor_copy(out=x_codes[1][:], in_=word_tables[1][:].bitcast(U32).indirect(offsets[:]))
+
+        w1_mx = {}
+        for g in range(h_passes):
+            for o in range(k_passes):
+                for t in range(PACK):
+                    name = "w1_%d_%d_%d" % (g, o, t)
+                    w1_mx[g, o, t] = (sbuf(name + "_codes", [P, P], U32), sbuf(name + "_scales", [P, P], U8))
+
+        def prepare_w1(index, engines):
+            g, o, first, width = pieces[index]
+            src = w1_raw[index][:].rearrange("p j (b t u v) -> p t b u j v", t=PACK, u=2, v=4)
+            cols = slice(first // PACK, (first + width) // PACK)
+            rounded = []
+
+            def quantize_tile(t):
+                codes, scales = w1_mx[g, o, t]
+                nc.vector.quantize_mx(out=codes[:, cols].bitcast(FP8X4), scales=scales[:, cols], in_=rounded[t][:])
+
+            for t in range(PACK):
+                rounded.append(sbuf("w1_bf16_%d_%d" % (index, t), [P, width], BF16))
+                dst = rounded[t][:].rearrange("p (b u v j) -> p b u j v", u=2, v=4, j=PACK)
+                copy_on(engines[t], dst, src[:, t])
+                if t > 0:
+                    quantize_tile(t - 1)
+            quantize_tile(PACK - 1)
+
+        def layer1_pass(bank, g, o, t, s):
+            codes, scales = w1_mx[g, o, t]
+            cols = slice(s * CHUNK, (s + 1) * CHUNK)
+            nc.tensor.matmul_mx(
+                out=bank[:, t * CHUNK : (t + 1) * CHUNK],
+                lhsT=codes[:].bitcast(FP8X4),
+                lhsT_scale=scales[:],
+                rhs=x_codes[o][:, cols].bitcast(FP8X4),
+                rhs_scale=x_bytes[4 * o : P, cols],
+                start=(o == 0),
+                stop=(o == k_passes - 1),
+            )
+
+        h_bf16 = {}
+        h_mx = {}
+
+        def relu_out(bank, g, s, engine, reuse=None):
+            hb = sbuf("h_bf16_%d_%d" % (g, s), [P, PASS], BF16, reuse)
+            dst = hb[:].rearrange("p (c t) -> p c t", t=PACK)
+            src = bank[:].rearrange("p (t c) -> p c t", t=PACK)
+            if engine == "vector":
+                nc.vector.tensor_scalar_max(dst, src, 0.0)
+            else:
+                nc.scalar.activation(out=dst, in_=src, func=RELU)
+            h_bf16[g, s] = hb
+
+        def new_bank(index):
+            return psum.tile([P, PASS], F32, name="bank%d" % index)
+
+        V, A = "vector", "scalar"
+        w2_mx = []
+
+        def prepare_w2(g, engine):
+            wb = sbuf("w2_bf16_%d" % g, [P, PASS], BF16)
+            copy_on(
+                engine,
+                wb[:].rearrange("p (c v t) -> p c t v", v=4, t=PACK),
+                w2_raw[g][:].rearrange("p t (c v) -> p c t v", v=4),
+            )
+            w2_mx.append(quantize("w2_%d" % g, wb))
+
+        prepare_w2(0, A)
+        prepare_w1(0, [V, V, A, A])
+        prepare_w1(1, [V, A, V, A])
+
+        banks0 = [new_bank(s) for s in range(chunks)]
+        for s in range(chunks):
+            for t in range(PACK):
+                for o in range(k_passes):
+                    layer1_pass(banks0[s], 0, o, t, s)
+            if s < chunks - 1:
+                relu_out(banks0[s], 0, s, A)
+
+        prepare_w1(2, [V, V, V, V])
+        prepare_w1(3, [V, V, V, V])
+        banks1 = [new_bank(chunks + s) for s in range(chunks)]
+        for s in range(chunks):
+            layer1_pass(banks1[s], 1, 0, 0, s)
+        prepare_w1(4, [V, V, V, V])
+        prepare_w1(5, [V, A, V, A])
+        relu_out(banks0[chunks - 1], 0, chunks - 1, A, "w1_raw_5")
+        for s in range(chunks):
+            h_mx[0, s] = quantize("h_0_%d" % s, h_bf16[0, s], "w1_bf16_5_%d" % s)
+        prepare_w2(1, V)
+
+        for s in range(chunks):
+            layer1_pass(banks1[s], 1, 1, 0, s)
+        for s in range(chunks):
+            for t in range(1, PACK):
+                for o in range(k_passes):
+                    layer1_pass(banks1[s], 1, o, t, s)
+            relu_out(banks1[s], 1, s, [A, V, A, A][s])
+
+        for s in range(chunks):
+            h_mx[1, s] = quantize("h_1_%d" % s, h_bf16[1, s])
+            acc = new_bank(s)
+            for g in range(h_passes):
+                nc.tensor.matmul_mx(
+                    out=acc[:, 0:CHUNK],
+                    lhsT=w2_mx[g][0][:].bitcast(FP8X4),
+                    lhsT_scale=w2_mx[g][1][:],
+                    rhs=h_mx[g, s][0][:].bitcast(FP8X4),
+                    rhs_scale=h_mx[g, s][1][:],
+                    start=(g == 0),
+                    stop=(g == h_passes - 1),
+                )
+            y = sbuf("y%d" % s, [P, CHUNK], F32)
+            copy_on(V, y[:], acc[:, 0:CHUNK])
+            nc.sync.dma_start(out[:, s * CHUNK : (s + 1) * CHUNK], y[:])

@@ -49,16 +49,23 @@ def tile_picked_pick_mlp_relu_sub_p_kernel(tc, x_words, x_scales, w1, w2, offs, 
             return codes, scales
 
         offsets = keep.tile([P, S // 16], U16, name="offsets")
+        nc.sync.dma_start(offsets[:], offs)
 
         scale_table = sbuf("scale_table", [P, T], U8)
         nc.vector.memset(scale_table[:].bitcast(I32), 0)
+
+        w2_raw = []
+
+        def load_w2(g):
+            raw = sbuf("w2_raw%d" % g, [P, PACK, N], F32)
+            nc.sync.dma_start(raw[:], w2[g * PASS : (g + 1) * PASS, :].rearrange("(p j) n -> p j n", j=PACK))
+            w2_raw.append(raw)
 
         word_tables = [sbuf("word_table%d" % o, [P, T], I32) for o in range(k_passes)]
 
         def load_words(o):
             nc.sync.dma_start(word_tables[o][:], x_words[o].rearrange("p c r -> p (c r)").bitcast(I32))
 
-        nc.sync.dma_start(offsets[:], offs)
         load_words(0)
         for quad in range(4):
             nc.sync.dma_start(
@@ -66,10 +73,10 @@ def tile_picked_pick_mlp_relu_sub_p_kernel(tc, x_words, x_scales, w1, w2, offs, 
                 x_scales[:, 4 * quad : 4 * quad + 4, :].bitcast(I32),
             )
         load_words(1)
+        load_w2(0)
 
-        pieces = [(0, 0, 0, PASS), (0, 1, 0, PASS), (1, 0, 0, HALF), (1, 0, HALF, HALF), (1, 1, 0, HALF), (1, 1, HALF, HALF)]
+        pieces = [(0, 0, 0, PASS), (0, 1, 0, HALF), (0, 1, HALF, HALF), (1, 0, 0, HALF), (1, 0, HALF, HALF), (1, 1, 0, HALF), (1, 1, HALF, HALF)]
         w1_raw = []
-        w2_raw = []
 
         def load_w1(g, o, first, width):
             raw = sbuf("w1_raw_%d" % len(w1_raw), [P, PACK, width], F32)
@@ -77,17 +84,9 @@ def tile_picked_pick_mlp_relu_sub_p_kernel(tc, x_words, x_scales, w1, w2, offs, 
             nc.sync.dma_start(raw[:], w1[o * PASS : (o + 1) * PASS, cols].rearrange("(p j) c -> p j c", j=PACK))
             w1_raw.append(raw)
 
-        def load_w2(g, queue):
-            raw = sbuf("w2_raw%d" % g, [P, PACK, N], F32)
-            rows = w2[g * PASS : (g + 1) * PASS, :].rearrange("(b t i) n -> t b i n", t=PACK, i=SUB)
-            for t in range(PACK):
-                queue.dma_start(raw[:, t, :], rows[t])
-            w2_raw.append(raw)
-
-        load_w2(0, nc.sync)
         for piece in pieces:
             load_w1(*piece)
-        load_w2(1, nc.sync)
+        load_w2(1)
 
         x_codes = [sbuf("x_codes%d" % o, [P, S], U32) for o in range(k_passes)]
         x_bytes = sbuf("x_bytes", [P, S], U8)
@@ -102,23 +101,19 @@ def tile_picked_pick_mlp_relu_sub_p_kernel(tc, x_words, x_scales, w1, w2, offs, 
                     name = "w1_%d_%d_%d" % (g, o, t)
                     w1_mx[g, o, t] = (sbuf(name + "_codes", [P, P], U32), sbuf(name + "_scales", [P, P], U8))
 
-        def prepare_w1(index, engines):
+        def prepare_w1(index, second_engine):
             g, o, first, width = pieces[index]
-            src = w1_raw[index][:].rearrange("p j (b t u v) -> p t b u j v", t=PACK, u=2, v=4)
+            src = w1_raw[index][:].rearrange("p j (m u e) -> p u m j e", u=2, e=2)
             cols = slice(first // PACK, (first + width) // PACK)
             rounded = []
-
-            def quantize_tile(t):
-                codes, scales = w1_mx[g, o, t]
-                nc.vector.quantize_mx(out=codes[:, cols].bitcast(FP8X4), scales=scales[:, cols], in_=rounded[t][:])
-
+            for u, engine in enumerate(["vector", second_engine]):
+                rounded.append(sbuf("w1_bf16_%d_%d" % (index, u), [P, 2, width], BF16))
+                copy_on(engine, rounded[u][:].rearrange("p e (m j) -> p m j e", j=PACK), src[:, u])
             for t in range(PACK):
-                rounded.append(sbuf("w1_bf16_%d_%d" % (index, t), [P, width], BF16))
-                dst = rounded[t][:].rearrange("p (b u v j) -> p b u j v", u=2, v=4, j=PACK)
-                copy_on(engines[t], dst, src[:, t])
-                if t > 0:
-                    quantize_tile(t - 1)
-            quantize_tile(PACK - 1)
+                codes, scales = w1_mx[g, o, t]
+                nc.vector.quantize_mx(
+                    out=codes[:, cols].bitcast(FP8X4), scales=scales[:, cols], in_=rounded[t // 2][:, t % 2, :]
+                )
 
         def layer1_pass(bank, g, o, t, s):
             codes, scales = w1_mx[g, o, t]
@@ -138,8 +133,8 @@ def tile_picked_pick_mlp_relu_sub_p_kernel(tc, x_words, x_scales, w1, w2, offs, 
 
         def relu_out(bank, g, s, engine, reuse=None):
             hb = sbuf("h_bf16_%d_%d" % (g, s), [P, PASS], BF16, reuse)
-            dst = hb[:].rearrange("p (c t) -> p c t", t=PACK)
-            src = bank[:].rearrange("p (t c) -> p c t", t=PACK)
+            dst = hb[:].rearrange("p (c e t) -> p c t e", e=2, t=PACK)
+            src = bank[:].rearrange("p (t c e) -> p c t e", e=2, t=PACK)
             if engine == "vector":
                 nc.vector.tensor_scalar_max(dst, src, 0.0)
             else:
@@ -162,27 +157,44 @@ def tile_picked_pick_mlp_relu_sub_p_kernel(tc, x_words, x_scales, w1, w2, offs, 
             w2_mx.append(quantize("w2_%d" % g, wb))
 
         prepare_w2(0, A)
-        prepare_w1(0, [V, V, A, A])
-        prepare_w1(1, [V, A, V, A])
+        prepare_w1(0, A)
+
+        def keep_busy(index, g, t):
+            unread = new_bank(index)
+            nc.tensor.matmul_mx(
+                out=unread[:],
+                lhsT=w1_mx[g, 0, t][0][:].bitcast(FP8X4),
+                lhsT_scale=w1_mx[g, 0, t][1][:],
+                rhs=x_codes[0][:].bitcast(FP8X4),
+                rhs_scale=x_bytes[:],
+                start=True,
+                stop=True,
+            )
+
+        keep_busy(chunks, 0, 0)
+        keep_busy(chunks + 1, 0, 0)
+        prepare_w1(1, A)
+        prepare_w1(2, A)
 
         banks0 = [new_bank(s) for s in range(chunks)]
+        banks1 = [new_bank(chunks + s) for s in range(chunks)]
         for s in range(chunks):
             for t in range(PACK):
                 for o in range(k_passes):
                     layer1_pass(banks0[s], 0, o, t, s)
             if s < chunks - 1:
                 relu_out(banks0[s], 0, s, A)
-
-        prepare_w1(2, [V, V, V, V])
-        prepare_w1(3, [V, V, V, V])
-        banks1 = [new_bank(chunks + s) for s in range(chunks)]
-        for s in range(chunks):
-            layer1_pass(banks1[s], 1, 0, 0, s)
-        prepare_w1(4, [V, V, V, V])
-        prepare_w1(5, [V, A, V, A])
-        relu_out(banks0[chunks - 1], 0, chunks - 1, A, "w1_raw_5")
-        for s in range(chunks):
-            h_mx[0, s] = quantize("h_0_%d" % s, h_bf16[0, s], "w1_bf16_5_%d" % s)
+        prepare_w1(3, V)
+        prepare_w1(4, V)
+        for bank in range(chunks):
+            layer1_pass(banks1[bank], 1, 0, 0, bank)
+        keep_busy(0, 1, PACK - 1)
+        keep_busy(1, 1, PACK - 1)
+        prepare_w1(5, A)
+        prepare_w1(6, A)
+        relu_out(banks0[3], 0, 3, A, "w1_raw_6")
+        for s, reuse in enumerate(["w1_bf16_6_1", "h_bf16_0_0", "h_bf16_0_1", "h_bf16_0_2"]):
+            h_mx[0, s] = quantize("h_0_%d" % s, h_bf16[0, s], reuse)
         prepare_w2(1, V)
 
         for s in range(chunks):

from contextlib import ExitStack

import concourse.mybir as mybir

K, T, S, H, N = 1024, 2048, 512, 1024, 128
FLOPS = 2 * K * H * S + 2 * H * N * S

F32 = mybir.dt.float32
BF16 = mybir.dt.bfloat16
I32 = mybir.dt.int32
U32 = mybir.dt.uint32
U16 = mybir.dt.uint16
U8 = mybir.dt.uint8
FP8X4 = mybir.dt.float8_e4m3fn_x4
RELU = mybir.ActivationFunctionType.Relu

P = 128
PACK = 4
PASS = P * PACK
BLOCK = 32
SUB = BLOCK // PACK
CHUNK = 128
HALF = PASS // 2


def tile_picked_pick_mlp_relu_sub_p_kernel(tc, x_words, x_scales, w1, w2, offs, out):
    nc = tc.nc
    k_passes = K // PASS
    h_passes = H // PASS
    chunks = S // CHUNK

    with ExitStack() as ctx:
        keep = ctx.enter_context(tc.tile_pool(name="keep", bufs=1))
        psum = ctx.enter_context(tc.psum_pool(name="psum", bufs=1))

        def sbuf(name, shape, dtype, reuse=None):
            return keep.tile(shape, dtype, name=name, tag=reuse or name, align_bytes=64)

        def copy_on(engine, dst, src):
            if engine == "vector":
                nc.vector.tensor_copy(out=dst, in_=src)
            else:
                nc.scalar.copy(out=dst, in_=src)

        def quantize(name, values, reuse=None):
            codes = sbuf(name + "_codes", [P, P], U32, reuse)
            scales = sbuf(name + "_scales", [P, P], U8)
            nc.vector.quantize_mx(out=codes[:].bitcast(FP8X4), scales=scales[:], in_=values[:])
            return codes, scales

        offsets = keep.tile([P, S // 16], U16, name="offsets")
        nc.sync.dma_start(offsets[:], offs)

        scale_table = sbuf("scale_table", [P, T], U8)
        nc.vector.memset(scale_table[:].bitcast(I32), 0)

        w2_raw = []

        def load_w2(g):
            raw = sbuf("w2_raw%d" % g, [P, PACK, N], F32)
            nc.sync.dma_start(raw[:], w2[g * PASS : (g + 1) * PASS, :].rearrange("(p j) n -> p j n", j=PACK))
            w2_raw.append(raw)

        word_tables = [sbuf("word_table%d" % o, [P, T], I32) for o in range(k_passes)]

        def load_words(o):
            nc.sync.dma_start(word_tables[o][:], x_words[o].rearrange("p c r -> p (c r)").bitcast(I32))

        load_words(0)
        for quad in range(4):
            nc.sync.dma_start(
                scale_table[32 * quad : 32 * quad + 4 * k_passes, :].bitcast(I32),
                x_scales[:, 4 * quad : 4 * quad + 4, :].bitcast(I32),
            )
        load_words(1)
        load_w2(0)

        pieces = [(0, 0, 0, PASS), (0, 1, 0, HALF), (0, 1, HALF, HALF), (1, 0, 0, HALF), (1, 0, HALF, HALF), (1, 1, 0, HALF), (1, 1, HALF, HALF)]
        w1_raw = []

        def load_w1(g, o, first, width):
            raw = sbuf("w1_raw_%d" % len(w1_raw), [P, PACK, width], F32)
            cols = slice(g * PASS + first, g * PASS + first + width)
            nc.sync.dma_start(raw[:], w1[o * PASS : (o + 1) * PASS, cols].rearrange("(p j) c -> p j c", j=PACK))
            w1_raw.append(raw)

        for piece in pieces:
            load_w1(*piece)
        load_w2(1)

        x_codes = [sbuf("x_codes%d" % o, [P, S], U32) for o in range(k_passes)]
        x_bytes = sbuf("x_bytes", [P, S], U8)
        nc.vector.tensor_copy(out=x_codes[0][:], in_=word_tables[0][:].bitcast(U32).indirect(offsets[:]))
        nc.vector.tensor_copy(out=x_bytes[:], in_=scale_table[:].indirect(offsets[:]))
        nc.vector.tensor_copy(out=x_codes[1][:], in_=word_tables[1][:].bitcast(U32).indirect(offsets[:]))

        w1_mx = {}
        for g in range(h_passes):
            for o in range(k_passes):
                for t in range(PACK):
                    name = "w1_%d_%d_%d" % (g, o, t)
                    w1_mx[g, o, t] = (sbuf(name + "_codes", [P, P], U32), sbuf(name + "_scales", [P, P], U8))

        def prepare_w1(index, second_engine):
            g, o, first, width = pieces[index]
            src = w1_raw[index][:].rearrange("p j (m u e) -> p u m j e", u=2, e=2)
            cols = slice(first // PACK, (first + width) // PACK)
            rounded = []
            for u, engine in enumerate(["vector", second_engine]):
                rounded.append(sbuf("w1_bf16_%d_%d" % (index, u), [P, 2, width], BF16))
                copy_on(engine, rounded[u][:].rearrange("p e (m j) -> p m j e", j=PACK), src[:, u])
            for t in range(PACK):
                codes, scales = w1_mx[g, o, t]
                nc.vector.quantize_mx(
                    out=codes[:, cols].bitcast(FP8X4), scales=scales[:, cols], in_=rounded[t // 2][:, t % 2, :]
                )

        def layer1_pass(bank, g, o, t, s):
            codes, scales = w1_mx[g, o, t]
            cols = slice(s * CHUNK, (s + 1) * CHUNK)
            nc.tensor.matmul_mx(
                out=bank[:, t * CHUNK : (t + 1) * CHUNK],
                lhsT=codes[:].bitcast(FP8X4),
                lhsT_scale=scales[:],
                rhs=x_codes[o][:, cols].bitcast(FP8X4),
                rhs_scale=x_bytes[4 * o : P, cols],
                start=(o == 0),
                stop=(o == k_passes - 1),
            )

        h_bf16 = {}
        h_mx = {}

        def relu_out(bank, g, s, engine, reuse=None):
            hb = sbuf("h_bf16_%d_%d" % (g, s), [P, PASS], BF16, reuse)
            dst = hb[:].rearrange("p (c e t) -> p c t e", e=2, t=PACK)
            src = bank[:].rearrange("p (t c e) -> p c t e", e=2, t=PACK)
            if engine == "vector":
                nc.vector.tensor_scalar_max(dst, src, 0.0)
            else:
                nc.scalar.activation(out=dst, in_=src, func=RELU)
            h_bf16[g, s] = hb

        def new_bank(index):
            return psum.tile([P, PASS], F32, name="bank%d" % index)

        V, A = "vector", "scalar"
        w2_mx = []

        def prepare_w2(g, engine):
            wb = sbuf("w2_bf16_%d" % g, [P, PASS], BF16)
            copy_on(
                engine,
                wb[:].rearrange("p (c v t) -> p c t v", v=4, t=PACK),
                w2_raw[g][:].rearrange("p t (c v) -> p c t v", v=4),
            )
            w2_mx.append(quantize("w2_%d" % g, wb))

        prepare_w2(0, A)
        prepare_w1(0, A)

        def keep_busy(index, g, t):
            unread = new_bank(index)
            nc.tensor.matmul_mx(
                out=unread[:],
                lhsT=w1_mx[g, 0, t][0][:].bitcast(FP8X4),
                lhsT_scale=w1_mx[g, 0, t][1][:],
                rhs=x_codes[0][:].bitcast(FP8X4),
                rhs_scale=x_bytes[:],
                start=True,
                stop=True,
            )

        keep_busy(chunks, 0, 0)
        keep_busy(chunks + 1, 0, 0)
        prepare_w1(1, A)
        prepare_w1(2, A)

        banks0 = [new_bank(s) for s in range(chunks)]
        banks1 = [new_bank(chunks + s) for s in range(chunks)]
        for s in range(chunks):
            for t in range(PACK):
                for o in range(k_passes):
                    layer1_pass(banks0[s], 0, o, t, s)
            if s < chunks - 1:
                relu_out(banks0[s], 0, s, A)
        prepare_w1(3, V)
        prepare_w1(4, V)
        for bank in range(chunks):
            layer1_pass(banks1[bank], 1, 0, 0, bank)
        keep_busy(0, 1, PACK - 1)
        keep_busy(1, 1, PACK - 1)
        prepare_w1(5, A)
        prepare_w1(6, A)
        relu_out(banks0[3], 0, 3, A, "w1_raw_6")
        for s, reuse in enumerate(["w1_bf16_6_1", "h_bf16_0_0", "h_bf16_0_1", "h_bf16_0_2"]):
            h_mx[0, s] = quantize("h_0_%d" % s, h_bf16[0, s], reuse)
        prepare_w2(1, V)

        for s in range(chunks):
            layer1_pass(banks1[s], 1, 1, 0, s)
        for s in range(chunks):
            for t in range(1, PACK):
                for o in range(k_passes):
                    layer1_pass(banks1[s], 1, o, t, s)
            relu_out(banks1[s], 1, s, [A, V, A, A][s])

        for s in range(chunks):
            h_mx[1, s] = quantize("h_1_%d" % s, h_bf16[1, s])
            acc = new_bank(s)
            for g in range(h_passes):
                nc.tensor.matmul_mx(
                    out=acc[:, 0:CHUNK],
                    lhsT=w2_mx[g][0][:].bitcast(FP8X4),
                    lhsT_scale=w2_mx[g][1][:],
                    rhs=h_mx[g, s][0][:].bitcast(FP8X4),
                    rhs_scale=h_mx[g, s][1][:],
                    start=(g == 0),
                    stop=(g == h_passes - 1),
                )
            y = sbuf("y%d" % s, [P, CHUNK], F32)
            copy_on(V, y[:], acc[:, 0:CHUNK])
            nc.sync.dma_start(out[:, s * CHUNK : (s + 1) * CHUNK], y[:])
